import numpy as np
import ml_dtypes


def mxq(x, axis, fmt="e4m3"):
    dtype, down = {"e4m3": (ml_dtypes.float8_e4m3fn, 7), "e5m2": (ml_dtypes.float8_e5m2, 14)}[fmt]
    v = np.moveaxis(np.asarray(x, np.float32).astype(ml_dtypes.bfloat16).astype(np.float64), axis, -1)
    blocks = v.reshape(v.shape[:-1] + (-1, 32))
    amax = np.abs(blocks).max(-1, keepdims=True)
    byte = np.maximum(np.where(amax > 0, np.frexp(amax)[1] - 1 + 127, 0) - down, 1)
    scale = np.exp2(byte - 127.0)
    codes = (blocks / scale).astype(np.float32).astype(dtype).astype(np.float64)
    return np.moveaxis((codes * scale).reshape(v.shape), -1, axis)


WIDE = False


def mx_kscale(k):
    if not WIDE:
        return np.ones(k)
    levels = np.array([30, -30])
    if k % 512:
        return np.exp2(np.random.permutation(np.resize(levels, k // 32))).repeat(32)
    a = np.empty((k // 512, 16))
    for p in range(k // 512):
        a[p, :8] = np.random.permutation(np.resize(levels, 8))
        for g in range(8):
            far = levels[np.abs(levels - a[p, g]) >= 10]
            a[p, g + 8] = far[np.random.randint(len(far))]
    return np.exp2(a.ravel()).repeat(32)


def f64(x):
    return np.asarray(x).astype(np.float64)


def striped(idx):
    return np.tile(np.asarray(idx).reshape(-1, 16).T, (8, 1)).astype(np.uint16)


def unstriped(offs):
    return offs[:16].T.reshape(-1).astype(np.int64)


E2M1 = np.array([0.0, 0.5, 1.0, 1.5, 2.0, 3.0, 4.0, 6.0, -0.0, -0.5, -1.0, -1.5, -2.0, -3.0, -4.0, -6.0])


def pack_weight(w, fmt):
    k, n = w.shape
    w = f64(np.asarray(w, np.float32).astype(ml_dtypes.bfloat16)).reshape(k // 32, 32, n)
    amax = np.abs(w).max(1)
    if fmt in ("e4m3", "e5m2"):
        byte = np.frexp(amax)[1] - 1 + 127 - (7 if fmt == "e4m3" else 14)
    else:
        mant, ex = np.frexp(amax / 6.0)
        byte = np.where(mant > 0.5, ex, ex - 1) + 127
    byte = np.clip(np.where(amax > 0, byte, 1), 1, 254)
    scaled = (w * np.exp2(127.0 - byte)[:, None, :]).reshape(k, n).astype(np.float32)
    by_word = np.ascontiguousarray(scaled.reshape(k // 512, 128, 4, n).transpose(0, 1, 3, 2))
    if fmt in ("e4m3", "e5m2"):
        words = by_word.astype(ml_dtypes.float8_e4m3fn if fmt == "e4m3" else ml_dtypes.float8_e5m2).view(np.uint8)
    else:
        c = by_word.astype(ml_dtypes.float4_e2m1fn).view(np.uint8) & 0xF
        words = (c[..., 0::2] | (c[..., 1::2] << 4)).reshape(k // 512, 128, 2 * n)
    return np.ascontiguousarray(words), np.ascontiguousarray(byte.astype(np.uint8).reshape(k // 512, 16, n))


def unpack_weight(words, scales, fmt):
    g, _, n = scales.shape
    words = np.ascontiguousarray(words).reshape(g, 128, n, -1)
    if fmt in ("e4m3", "e5m2"):
        vals = words.view(ml_dtypes.float8_e4m3fn if fmt == "e4m3" else ml_dtypes.float8_e5m2).astype(np.float64)
    else:
        nib = np.empty((g, 128, n, 4), np.uint8)
        nib[..., 0::2] = words & 0xF
        nib[..., 1::2] = words >> 4
        vals = E2M1[nib]
    vals = vals * np.repeat(np.exp2(scales.astype(np.float64) - 127.0), 8, axis=1)[..., None]
    return vals.transpose(0, 1, 3, 2).reshape(g * 512, n)


K, T, J, I, R, C, Q = 512, 512, 256, 256, 512, 512, 1024


def setup_inputs():
    n = np.random.standard_normal
    idx = np.random.permutation(T)[:J]
    idx2 = np.random.permutation(T)[:I]
    idx3 = np.random.permutation(C)[:I]
    idx4 = np.random.permutation(Q)[:I]
    fk = mx_kscale(K)
    fr = mx_kscale(R)
    xtp = pack_weight(n((K, T)) / fk[:, None], "e4m3")
    wap = pack_weight(n((K, R)) * 0.5 / np.sqrt(K) * fk[:, None] * fr, "e2m1")
    wbp = pack_weight(n((K, R)) * 1 / np.sqrt(K) * fk[:, None] / fr, "e5m2")
    return {
        "xt_words": xtp[0],
        "xt_scales": xtp[1],
        "wa_words": wap[0],
        "wa_scales": wap[1],
        "wb_words": wbp[0],
        "wb_scales": wbp[1],
        "tf": (n((R, C))).astype(np.float32),
        "old": (10.0 * n((J, Q))).astype(np.float32),
        "offs": striped(idx),
        "offs2": striped(idx2),
        "offs3": striped(idx3),
        "offs4": striped(idx4),
    }


def reference(xt_words, xt_scales, wa_words, wa_scales, wb_words, wb_scales, tf, old, offs, offs2, offs3, offs4):
    idx = unstriped(offs)
    idx2 = unstriped(offs2)
    idx3 = unstriped(offs3)
    idx4 = unstriped(offs4)
    xtu = unpack_weight(xt_words, xt_scales, "e4m3")
    wau = unpack_weight(wa_words, wa_scales, "e2m1")
    wbu = unpack_weight(wb_words, wb_scales, "e5m2")
    xtidxg = xtu[:, idx]
    za = wau.T @ xtidxg
    ka1 = np.max(za, axis=1, keepdims=True)
    ha = np.maximum(za - 0.4 * ka1, 0.0)
    xtidx2g = xtu[:, idx2]
    zb = wbu.T @ xtidx2g
    hb = zb * f64(tf)[:, idx3]
    haq = mxq(ha, 0, "e4m3")
    hbq = mxq(hb, 0, "e5m2")
    a0 = haq.T @ hbq
    pp = np.zeros((J, Q))
    pp[:, idx4] = a0
    y = 0.04 * (pp - f64(old))
    return y

@@ -1,0 +1,191 @@
+from contextlib import ExitStack
+
+import concourse.mybir as mybir
+
+K, T, J, I, R, C, Q = 512, 512, 256, 256, 512, 512, 1024
+FLOPS = 2 * K * R * J + 2 * K * R * I + 2 * R * J * I
+
+F32 = mybir.dt.float32
+BF16 = mybir.dt.bfloat16
+I32 = mybir.dt.int32
+U32 = mybir.dt.uint32
+U16 = mybir.dt.uint16
+U8 = mybir.dt.uint8
+E4M3 = mybir.dt.float8_e4m3fn_x4
+E5M2 = mybir.dt.float8_e5m2_x4
+E2M1 = mybir.dt.float4_e2m1fn_x4
+ALU = mybir.AluOpType
+ACT = mybir.ActivationFunctionType
+
+P = 128
+PACK = 4
+HALF = 128
+
+
+def tile_list_meet_peakgated_timestable_placed_kernel(
+    tc, xt_words, xt_scales, wa_words, wa_scales, wb_words, wb_scales, tf, old, offs, offs2, offs3, offs4, out
+):
+    nc = tc.nc
+    with ExitStack() as ctx:
+        sb = ctx.enter_context(tc.tile_pool(name="sb", bufs=1))
+        ps = ctx.enter_context(tc.psum_pool(name="ps", bufs=1))
+
+        def load_list(src, name):
+            t = sb.tile([P, 16], U16, name=name)
+            nc.sync.dma_start(t[:], src)
+            return t
+
+        def load_scales(src, name, queue):
+            t = sb.tile([P, 512], U8, name=name, align_bytes=64)
+            rows = src[0].bitcast(I32)
+            for quad in range(4):
+                four = rows[4 * quad : 4 * quad + 4, :].unsqueeze(0).broadcast_to([8, 4, 128])
+                queue.dma_start(t[32 * quad : 32 * quad + 32, :].bitcast(I32), four)
+            return t
+
+        tf_rows = tf.rearrange("(g t e) c -> t g e c", t=4, e=8)
+        tf_sb = [sb.tile([P, C], F32, name="tf%d" % t) for t in range(PACK)]
+
+        list_j = load_list(offs, "list_j")
+        xt_w = sb.tile([P, T], I32, name="xt_w", align_bytes=64)
+        nc.sync.dma_start(xt_w[:], xt_words[0].rearrange("p n t -> p (n t)").bitcast(I32))
+        xt_s = load_scales(xt_scales, "xt_s", nc.scalar)
+        list_c = load_list(offs3, "list_c")
+        nc.sync.dma_start(tf_sb[0][:], tf_rows[0])
+        list_i = load_list(offs2, "list_i")
+        wa_w = sb.tile([P, R // 2], I32, name="wa_w", align_bytes=64)
+        nc.sync.dma_start(wa_w[:], wa_words[0].bitcast(I32))
+        wa_s = load_scales(wa_scales, "wa_s", nc.sync)
+        nc.sync.dma_start(tf_sb[1][:], tf_rows[1])
+        wb_w = sb.tile([P, R], I32, name="wb_w", align_bytes=64)
+        nc.sync.dma_start(wb_w[:], wb_words[0].rearrange("p n t -> p (n t)").bitcast(I32))
+        nc.sync.dma_start(tf_sb[2][:], tf_rows[2])
+        nc.sync.dma_start(tf_sb[3][:], tf_rows[3])
+        wb_s = load_scales(wb_scales, "wb_s", nc.sync)
+        list_q = load_list(offs4, "list_q")
+        old_sb = [sb.tile([P, Q], F32, name="old%d" % h) for h in range(2)]
+        for h in range(2):
+            nc.sync.dma_start(old_sb[h][:], old[h * P : (h + 1) * P, :])
+
+        board = [sb.tile([P, Q], F32, name="board%d" % h) for h in range(2)]
+        for h in range(2):
+            nc.gpsimd.memset(board[h][:], 0.0)
+
+        def gather_tokens(lst, name):
+            w = sb.tile([P, 256], U32, name=name + "_w", align_bytes=64)
+            s = sb.tile([P, 256], U8, name=name + "_s", align_bytes=64)
+            nc.vector.tensor_copy(w[:], xt_w[:].bitcast(U32).indirect(lst[:]))
+            nc.vector.tensor_copy(s[:], xt_s[:].indirect(lst[:]))
+            return w, s
+
+        def deal(src, words, name, dtype, cols):
+            dst = sb.tile([P, cols], dtype, name=name, align_bytes=64)
+            nc.vector.tensor_copy(
+                dst[:].bitcast(I32).rearrange("p (t q b) -> p t q b", t=4, b=words),
+                src[:].bitcast(I32).rearrange("p (q t b) -> p t q b", t=4, b=words),
+            )
+            return dst
+
+        xa_w, xa_s = gather_tokens(list_j, "xa")
+        wa_d = deal(wa_w, 4, "wa_d", U8, 2 * R)
+        wa_ds = deal(wa_s, 2, "wa_ds", U8, R)
+        za = [ps.tile([P, J], F32, name="za%d" % t) for t in range(PACK)]
+        for t in range(PACK):
+            nc.tensor.matmul_mx(
+                out=za[t][:],
+                lhsT=wa_d[:, 2 * P * t : 2 * P * (t + 1)].bitcast(E2M1),
+                lhsT_scale=wa_ds[:, P * t : P * (t + 1)],
+                rhs=xa_w[:].bitcast(E4M3),
+                rhs_scale=xa_s[:],
+                start=True,
+                stop=True,
+            )
+
+        xb_w, xb_s = gather_tokens(list_i, "xb")
+        wb_d = deal(wb_w, 8, "wb_d", U32, R)
+        wb_ds = deal(wb_s, 2, "wb_ds", U8, R)
+        zb = [ps.tile([P, PACK, HALF], F32, name="zb%d" % u) for u in range(2)]
+        for u in range(2):
+            for t in range(PACK):
+                nc.tensor.matmul_mx(
+                    out=zb[u][:, t, :],
+                    lhsT=wb_d[:, P * t : P * (t + 1)].bitcast(E5M2),
+                    lhsT_scale=wb_ds[:, P * t : P * (t + 1)],
+                    rhs=xb_w[:, HALF * u : HALF * (u + 1)].bitcast(E4M3),
+                    rhs_scale=xb_s[:, HALF * u : HALF * (u + 1)],
+                    start=True,
+                    stop=True,
+                )
+
+        tfg = sb.tile([P, PACK, I], F32, name="tfg")
+        for t in range(PACK):
+            nc.scalar.activation(tfg[:, t, :], tf_sb[t][:].indirect(list_c[:]), ACT.Copy)
+
+        ha_rows = sb.tile([P, PACK, J], BF16, name="ha_rows")
+        scaled = sb.tile([P, PACK, J], F32, name="scaled")
+        for t in range(PACK):
+            neg_cut = sb.tile([P, 1], F32, name="neg_cut%d" % t)
+            nc.vector.tensor_scalar(scaled[:, t, :], za[t][:], -0.4, None, ALU.mult, ALU.min, accum_out=neg_cut[:])
+            nc.scalar.activation(ha_rows[:, t, :], za[t][:], ACT.Relu, bias=neg_cut[:])
+
+        hb_bf = [sb.tile([P, HALF * PACK], BF16, name="hb_bf%d" % u, align_bytes=64) for u in range(2)]
+        hb_w = [sb.tile([P, HALF], U32, name="hb_w%d" % u, align_bytes=64) for u in range(2)]
+        hb_s = [sb.tile([P, HALF], U8, name="hb_s%d" % u, align_bytes=64) for u in range(2)]
+
+        def make_hb(u):
+            nc.vector.tensor_tensor(
+                hb_bf[u][:].rearrange("p (c i t) -> p c t i", i=4, t=4),
+                zb[u][:].rearrange("p t (c i) -> p c t i", i=4),
+                tfg[:, :, HALF * u : HALF * (u + 1)].rearrange("p t (c i) -> p c t i", i=4),
+                ALU.mult,
+            )
+
+        def quantise_hb(u):
+            nc.vector.quantize_mx(out=hb_w[u][:].bitcast(E5M2), scales=hb_s[u][:], in_=hb_bf[u][:])
+
+        make_hb(0)
+        ha_bf = sb.tile([P, J * PACK], BF16, name="ha_bf", align_bytes=64)
+        nc.vector.tensor_copy(
+            ha_bf[:].rearrange("p (c i t) -> p c t i", i=4, t=4),
+            ha_rows[:].rearrange("p t (c i) -> p c t i", i=4),
+        )
+        quantise_hb(0)
+        ha_w = sb.tile([P, J], U32, name="ha_w", align_bytes=64)
+        ha_s = sb.tile([P, J], U8, name="ha_s", align_bytes=64)
+        nc.vector.quantize_mx(out=ha_w[:].bitcast(E4M3), scales=ha_s[:], in_=ha_bf[:])
+
+        a0 = [ps.tile([P, 2, HALF], F32, name="a0_%d" % u) for u in range(2)]
+        a0_sb = [sb.tile([P, 2, HALF], F32, name="a0_sb%d" % u) for u in range(2)]
+
+        def scores(u):
+            for h in range(2):
+                nc.tensor.matmul_mx(
+                    out=a0[u][:, h, :],
+                    lhsT=ha_w[:, P * h : P * (h + 1)].bitcast(E4M3),
+                    lhsT_scale=ha_s[:, P * h : P * (h + 1)],
+                    rhs=hb_w[u][:].bitcast(E5M2),
+                    rhs_scale=hb_s[u][:],
+                    start=True,
+                    stop=True,
+                )
+
+        def places(h, u):
+            return board[h][:].indirect(list_q[:, 8 * u : 8 * (u + 1)])
+
+        scores(0)
+        nc.scalar.activation(a0_sb[0][:], a0[0][:], ACT.Copy, scale=0.04)
+        for h in range(2):
+            nc.scalar.activation(places(h, 0), a0_sb[0][:, h, :], ACT.Copy)
+        make_hb(1)
+        quantise_hb(1)
+        scores(1)
+        nc.vector.tensor_scalar(a0_sb[1][:], a0[1][:], 0.04, None, ALU.mult)
+        nc.vector.tensor_copy(places(0, 1), a0_sb[1][:, 0, :])
+        nc.scalar.activation(places(1, 1), a0_sb[1][:, 1, :], ACT.Copy)
+
+        for h in range(2):
+            for c0 in range(0, Q, 512):
+                cols = slice(c0, c0 + 512)
+                res = sb.tile([P, 512], F32, name="res%d_%d" % (h, c0))
+                nc.vector.scalar_tensor_tensor(res[:], old_sb[h][:, cols], -0.04, board[h][:, cols], ALU.mult, ALU.add)
+                nc.sync.dma_start(out[h * P : (h + 1) * P, cols], res[:])

@@ -36,7 +36,7 @@ def tile_list_meet_peakgated_timestable_placed_kernel(
             return t
 
         def load_scales(src, name, queue):
-            t = sb.tile([P, 512], U8, name=name, align_bytes=64)
+            t = sb.tile([P, 512], U8, name=name, tag=name, align_bytes=64)
             rows = src[0].bitcast(I32)
             for quad in range(4):
                 four = rows[4 * quad : 4 * quad + 4, :].unsqueeze(0).broadcast_to([8, 4, 128])
@@ -49,17 +49,17 @@ def tile_list_meet_peakgated_timestable_placed_kernel(
         list_j = load_list(offs, "list_j")
         xt_w = sb.tile([P, T], I32, name="xt_w", align_bytes=64)
         nc.sync.dma_start(xt_w[:], xt_words[0].rearrange("p n t -> p (n t)").bitcast(I32))
-        xt_s = load_scales(xt_scales, "xt_s", nc.scalar)
-        list_c = load_list(offs3, "list_c")
-        nc.sync.dma_start(tf_sb[0][:], tf_rows[0])
         list_i = load_list(offs2, "list_i")
+        xt_s = load_scales(xt_scales, "xt_s", nc.sync)
+        nc.sync.dma_start(tf_sb[0][:], tf_rows[0])
+        list_c = load_list(offs3, "list_c")
         wa_w = sb.tile([P, R // 2], I32, name="wa_w", align_bytes=64)
         nc.sync.dma_start(wa_w[:], wa_words[0].bitcast(I32))
         wa_s = load_scales(wa_scales, "wa_s", nc.sync)
         nc.sync.dma_start(tf_sb[1][:], tf_rows[1])
+        nc.sync.dma_start(tf_sb[2][:], tf_rows[2])
         wb_w = sb.tile([P, R], I32, name="wb_w", align_bytes=64)
         nc.sync.dma_start(wb_w[:], wb_words[0].rearrange("p n t -> p (n t)").bitcast(I32))
-        nc.sync.dma_start(tf_sb[2][:], tf_rows[2])
         nc.sync.dma_start(tf_sb[3][:], tf_rows[3])
         wb_s = load_scales(wb_scales, "wb_s", nc.sync)
         list_q = load_list(offs4, "list_q")
@@ -87,6 +87,7 @@ def tile_list_meet_peakgated_timestable_placed_kernel(
             return dst
 
         xa_w, xa_s = gather_tokens(list_j, "xa")
+        xb_w, xb_s = gather_tokens(list_i, "xb")
         wa_d = deal(wa_w, 4, "wa_d", U8, 2 * R)
         wa_ds = deal(wa_s, 2, "wa_ds", U8, R)
         za = [ps.tile([P, J], F32, name="za%d" % t) for t in range(PACK)]
@@ -101,7 +102,6 @@ def tile_list_meet_peakgated_timestable_placed_kernel(
                 stop=True,
             )
 
-        xb_w, xb_s = gather_tokens(list_i, "xb")
         wb_d = deal(wb_w, 8, "wb_d", U32, R)
         wb_ds = deal(wb_s, 2, "wb_ds", U8, R)
         zb = [ps.tile([P, PACK, HALF], F32, name="zb%d" % u) for u in range(2)]
@@ -121,33 +121,33 @@ def tile_list_meet_peakgated_timestable_placed_kernel(
         for t in range(PACK):
             nc.scalar.activation(tfg[:, t, :], tf_sb[t][:].indirect(list_c[:]), ACT.Copy)
 
-        ha_rows = sb.tile([P, PACK, J], BF16, name="ha_rows")
+        ha_rows = sb.tile([P, PACK, J], F32, name="ha_rows")
         scaled = sb.tile([P, PACK, J], F32, name="scaled")
         for t in range(PACK):
             neg_cut = sb.tile([P, 1], F32, name="neg_cut%d" % t)
             nc.vector.tensor_scalar(scaled[:, t, :], za[t][:], -0.4, None, ALU.mult, ALU.min, accum_out=neg_cut[:])
             nc.scalar.activation(ha_rows[:, t, :], za[t][:], ACT.Relu, bias=neg_cut[:])
 
-        hb_bf = [sb.tile([P, HALF * PACK], BF16, name="hb_bf%d" % u, align_bytes=64) for u in range(2)]
+        hb_bf = sb.tile([P, HALF * PACK], BF16, name="hb_bf", align_bytes=64)
         hb_w = [sb.tile([P, HALF], U32, name="hb_w%d" % u, align_bytes=64) for u in range(2)]
         hb_s = [sb.tile([P, HALF], U8, name="hb_s%d" % u, align_bytes=64) for u in range(2)]
 
         def make_hb(u):
             nc.vector.tensor_tensor(
-                hb_bf[u][:].rearrange("p (c i t) -> p c t i", i=4, t=4),
-                zb[u][:].rearrange("p t (c i) -> p c t i", i=4),
-                tfg[:, :, HALF * u : HALF * (u + 1)].rearrange("p t (c i) -> p c t i", i=4),
+                hb_bf[:].rearrange("p (c i t) -> p c t i", i=2, t=4),
+                zb[u][:].rearrange("p t (c i) -> p c t i", i=2),
+                tfg[:, :, HALF * u : HALF * (u + 1)].rearrange("p t (c i) -> p c t i", i=2),
                 ALU.mult,
             )
 
         def quantise_hb(u):
-            nc.vector.quantize_mx(out=hb_w[u][:].bitcast(E5M2), scales=hb_s[u][:], in_=hb_bf[u][:])
+            nc.vector.quantize_mx(out=hb_w[u][:].bitcast(E5M2), scales=hb_s[u][:], in_=hb_bf[:])
 
         make_hb(0)
-        ha_bf = sb.tile([P, J * PACK], BF16, name="ha_bf", align_bytes=64)
+        ha_bf = sb.tile([P, J * PACK], BF16, name="ha_bf", tag="wb_s", align_bytes=64)
         nc.vector.tensor_copy(
-            ha_bf[:].rearrange("p (c i t) -> p c t i", i=4, t=4),
-            ha_rows[:].rearrange("p t (c i) -> p c t i", i=4),
+            ha_bf[:].rearrange("p (c i t) -> p c t i", i=2, t=4),
+            ha_rows[:].rearrange("p t (c i) -> p c t i", i=2),
         )
         quantise_hb(0)
         ha_w = sb.tile([P, J], U32, name="ha_w", align_bytes=64)
@@ -155,7 +155,7 @@ def tile_list_meet_peakgated_timestable_placed_kernel(
         nc.vector.quantize_mx(out=ha_w[:].bitcast(E4M3), scales=ha_s[:], in_=ha_bf[:])
 
         a0 = [ps.tile([P, 2, HALF], F32, name="a0_%d" % u) for u in range(2)]
-        a0_sb = [sb.tile([P, 2, HALF], F32, name="a0_sb%d" % u) for u in range(2)]
+        a0_sb = sb.tile([P, 2, I], F32, name="a0_sb")
 
         def scores(u):
             for h in range(2):
@@ -169,23 +169,28 @@ def tile_list_meet_peakgated_timestable_placed_kernel(
                     stop=True,
                 )
 
-        def places(h, u):
-            return board[h][:].indirect(list_q[:, 8 * u : 8 * (u + 1)])
+        def leave_psum(u):
+            nc.scalar.activation(a0_sb[:, :, HALF * u : HALF * (u + 1)], a0[u][:], ACT.Copy, scale=0.04)
+
+        def place_upper(u):
+            nc.vector.tensor_copy(
+                board[0][:].indirect(list_q[:, 8 * u : 8 * (u + 1)]), a0_sb[:, 0, HALF * u : HALF * (u + 1)]
+            )
 
         scores(0)
-        nc.scalar.activation(a0_sb[0][:], a0[0][:], ACT.Copy, scale=0.04)
-        for h in range(2):
-            nc.scalar.activation(places(h, 0), a0_sb[0][:, h, :], ACT.Copy)
+        leave_psum(0)
         make_hb(1)
         quantise_hb(1)
+        place_upper(0)
         scores(1)
-        nc.vector.tensor_scalar(a0_sb[1][:], a0[1][:], 0.04, None, ALU.mult)
-        nc.vector.tensor_copy(places(0, 1), a0_sb[1][:, 0, :])
-        nc.scalar.activation(places(1, 1), a0_sb[1][:, 1, :], ACT.Copy)
+        leave_psum(1)
+        place_upper(1)
+        nc.scalar.activation(board[1][:].indirect(list_q[:]), a0_sb[:, 1, :], ACT.Copy)
 
-        for h in range(2):
-            for c0 in range(0, Q, 512):
-                cols = slice(c0, c0 + 512)
-                res = sb.tile([P, 512], F32, name="res%d_%d" % (h, c0))
+        for h, widths in ((0, (512, 512)), (1, (512, 512))):
+            for n, width in enumerate(widths):
+                c0 = sum(widths[:n])
+                cols = slice(c0, c0 + width)
+                res = sb.tile([P, width], F32, name="res%d_%d" % (h, c0))
                 nc.vector.scalar_tensor_tensor(res[:], old_sb[h][:, cols], -0.04, board[h][:, cols], ALU.mult, ALU.add)
                 nc.sync.dma_start(out[h * P : (h + 1) * P, cols], res[:])

@@ -46,9 +46,9 @@ def tile_list_meet_peakgated_timestable_placed_kernel(
         tf_rows = tf.rearrange("(g t e) c -> t g e c", t=4, e=8)
         tf_sb = [sb.tile([P, C], F32, name="tf%d" % t) for t in range(PACK)]
 
-        list_j = load_list(offs, "list_j")
         xt_w = sb.tile([P, T], I32, name="xt_w", align_bytes=64)
         nc.sync.dma_start(xt_w[:], xt_words[0].rearrange("p n t -> p (n t)").bitcast(I32))
+        list_j = load_list(offs, "list_j")
         list_i = load_list(offs2, "list_i")
         xt_s = load_scales(xt_scales, "xt_s", nc.sync)
         nc.sync.dma_start(tf_sb[0][:], tf_rows[0])
@@ -71,12 +71,15 @@ def tile_list_meet_peakgated_timestable_placed_kernel(
         for h in range(2):
             nc.gpsimd.memset(board[h][:], 0.0)
 
-        def gather_tokens(lst, name):
-            w = sb.tile([P, 256], U32, name=name + "_w", align_bytes=64)
-            s = sb.tile([P, 256], U8, name=name + "_s", align_bytes=64)
+        def gather_words(lst, name):
+            w = sb.tile([P, 256], U32, name=name, align_bytes=64)
             nc.vector.tensor_copy(w[:], xt_w[:].bitcast(U32).indirect(lst[:]))
+            return w
+
+        def gather_scales(lst, name, tag):
+            s = sb.tile([P, 256], U8, name=name, tag=tag, align_bytes=64)
             nc.vector.tensor_copy(s[:], xt_s[:].indirect(lst[:]))
-            return w, s
+            return s
 
         def deal(src, words, name, dtype, cols):
             dst = sb.tile([P, cols], dtype, name=name, align_bytes=64)
@@ -86,8 +89,9 @@ def tile_list_meet_peakgated_timestable_placed_kernel(
             )
             return dst
 
-        xa_w, xa_s = gather_tokens(list_j, "xa")
-        xb_w, xb_s = gather_tokens(list_i, "xb")
+        xa_w = gather_words(list_j, "xa_w")
+        xa_s = gather_scales(list_j, "xa_s", "xa_s")
+        xb_w = gather_words(list_i, "xb_w")
         wa_d = deal(wa_w, 4, "wa_d", U8, 2 * R)
         wa_ds = deal(wa_s, 2, "wa_ds", U8, R)
         za = [ps.tile([P, J], F32, name="za%d" % t) for t in range(PACK)]
@@ -102,6 +106,7 @@ def tile_list_meet_peakgated_timestable_placed_kernel(
                 stop=True,
             )
 
+        xb_s = gather_scales(list_i, "xb_s", "wa_s")
         wb_d = deal(wb_w, 8, "wb_d", U32, R)
         wb_ds = deal(wb_s, 2, "wb_ds", U8, R)
         zb = [ps.tile([P, PACK, HALF], F32, name="zb%d" % u) for u in range(2)]
@@ -117,16 +122,28 @@ def tile_list_meet_peakgated_timestable_placed_kernel(
                     stop=True,
                 )
 
-        tfg = sb.tile([P, PACK, I], F32, name="tfg")
-        for t in range(PACK):
-            nc.scalar.activation(tfg[:, t, :], tf_sb[t][:].indirect(list_c[:]), ACT.Copy)
+        tfg = [
+            sb.tile([P, PACK, HALF], F32, name="tfg0", tag="tfg0"),
+            None,
+        ]
+
+        def gather_factors(u, t):
+            nc.scalar.activation(tfg[u][:, t, :], tf_sb[t][:].indirect(list_c[:, 8 * u : 8 * (u + 1)]), ACT.Copy)
+
+        for t in range(PACK - 1):
+            gather_factors(0, t)
 
         ha_rows = sb.tile([P, PACK, J], F32, name="ha_rows")
         scaled = sb.tile([P, PACK, J], F32, name="scaled")
         for t in range(PACK):
-            neg_cut = sb.tile([P, 1], F32, name="neg_cut%d" % t)
+            neg_cut = sb.tile([P, 1], F32, name="neg_cut%d" % t, tag="neg_cut%d" % t)
             nc.vector.tensor_scalar(scaled[:, t, :], za[t][:], -0.4, None, ALU.mult, ALU.min, accum_out=neg_cut[:])
             nc.scalar.activation(ha_rows[:, t, :], za[t][:], ACT.Relu, bias=neg_cut[:])
+
+        gather_factors(0, PACK - 1)
+        tfg[1] = sb.tile([P, PACK, HALF], F32, name="tfg1", tag="neg_cut3")
+        for t in range(PACK):
+            gather_factors(1, t)
 
         hb_bf = sb.tile([P, HALF * PACK], BF16, name="hb_bf", align_bytes=64)
         hb_w = [sb.tile([P, HALF], U32, name="hb_w%d" % u, align_bytes=64) for u in range(2)]
@@ -136,7 +153,7 @@ def tile_list_meet_peakgated_timestable_placed_kernel(
             nc.vector.tensor_tensor(
                 hb_bf[:].rearrange("p (c i t) -> p c t i", i=2, t=4),
                 zb[u][:].rearrange("p t (c i) -> p c t i", i=2),
-                tfg[:, :, HALF * u : HALF * (u + 1)].rearrange("p t (c i) -> p c t i", i=2),
+                tfg[u][:].rearrange("p t (c i) -> p c t i", i=2),
                 ALU.mult,
             )
 

@@ -43,6 +43,14 @@ def tile_list_meet_peakgated_timestable_placed_kernel(
                 queue.dma_start(t[32 * quad : 32 * quad + 32, :].bitcast(I32), four)
             return t
 
+        def load_weight_scales(src, name):
+            t = sb.tile([P, 512], U8, name=name, tag=name, align_bytes=64)
+            nc.vector.memset(t[:].bitcast(I32), 0)
+            rows = src[0].bitcast(I32)
+            for quad in range(4):
+                nc.sync.dma_start(t[32 * quad : 32 * quad + 4, :].bitcast(I32), rows[4 * quad : 4 * quad + 4, :])
+            return t
+
         tf_rows = tf.rearrange("(g t e) c -> t g e c", t=4, e=8)
         tf_sb = [sb.tile([P, C], F32, name="tf%d" % t) for t in range(PACK)]
 
@@ -55,13 +63,13 @@ def tile_list_meet_peakgated_timestable_placed_kernel(
         list_c = load_list(offs3, "list_c")
         wa_w = sb.tile([P, R // 2], I32, name="wa_w", align_bytes=64)
         nc.sync.dma_start(wa_w[:], wa_words[0].bitcast(I32))
-        wa_s = load_scales(wa_scales, "wa_s", nc.sync)
+        wa_s = load_weight_scales(wa_scales, "wa_s")
         nc.sync.dma_start(tf_sb[1][:], tf_rows[1])
         nc.sync.dma_start(tf_sb[2][:], tf_rows[2])
         wb_w = sb.tile([P, R], I32, name="wb_w", align_bytes=64)
         nc.sync.dma_start(wb_w[:], wb_words[0].rearrange("p n t -> p (n t)").bitcast(I32))
         nc.sync.dma_start(tf_sb[3][:], tf_rows[3])
-        wb_s = load_scales(wb_scales, "wb_s", nc.sync)
+        wb_s = load_weight_scales(wb_scales, "wb_s")
         list_q = load_list(offs4, "list_q")
         old_sb = [sb.tile([P, Q], F32, name="old%d" % h) for h in range(2)]
         for h in range(2):
@@ -94,7 +102,7 @@ def tile_list_meet_peakgated_timestable_placed_kernel(
         xb_w = gather_words(list_i, "xb_w")
         wa_d = deal(wa_w, 4, "wa_d", U8, 2 * R)
         wa_ds = deal(wa_s, 2, "wa_ds", U8, R)
-        za = [ps.tile([P, J], F32, name="za%d" % t) for t in range(PACK)]
+        za = [ps.tile([P, J], F32, name="za%d" % t, tag="bank%d" % t) for t in range(PACK)]
         for t in range(PACK):
             nc.tensor.matmul_mx(
                 out=za[t][:],
@@ -171,13 +179,17 @@ def tile_list_meet_peakgated_timestable_placed_kernel(
         ha_s = sb.tile([P, J], U8, name="ha_s", align_bytes=64)
         nc.vector.quantize_mx(out=ha_w[:].bitcast(E4M3), scales=ha_s[:], in_=ha_bf[:])
 
-        a0 = [ps.tile([P, 2, HALF], F32, name="a0_%d" % u) for u in range(2)]
+        first_bank = ps.tile([P, 2, HALF], F32, name="a0_first")
+        a0 = [
+            [first_bank[:, h, :] for h in range(2)],
+            [ps.tile([P, HALF], F32, name="a0_second%d" % h, tag="bank%d" % h)[:] for h in range(2)],
+        ]
         a0_sb = sb.tile([P, 2, I], F32, name="a0_sb")
 
         def scores(u):
             for h in range(2):
                 nc.tensor.matmul_mx(
-                    out=a0[u][:, h, :],
+                    out=a0[u][h],
                     lhsT=ha_w[:, P * h : P * (h + 1)].bitcast(E4M3),
                     lhsT_scale=ha_s[:, P * h : P * (h + 1)],
                     rhs=hb_w[u][:].bitcast(E5M2),
@@ -186,21 +198,19 @@ def tile_list_meet_peakgated_timestable_placed_kernel(
                     stop=True,
                 )
 
-        def leave_psum(u):
-            nc.scalar.activation(a0_sb[:, :, HALF * u : HALF * (u + 1)], a0[u][:], ACT.Copy, scale=0.04)
-
         def place_upper(u):
             nc.vector.tensor_copy(
                 board[0][:].indirect(list_q[:, 8 * u : 8 * (u + 1)]), a0_sb[:, 0, HALF * u : HALF * (u + 1)]
             )
 
         scores(0)
-        leave_psum(0)
+        nc.scalar.activation(a0_sb[:, :, :HALF], first_bank[:], ACT.Copy, scale=0.04)
         make_hb(1)
         quantise_hb(1)
         place_upper(0)
         scores(1)
-        leave_psum(1)
+        for h in range(2):
+            nc.scalar.activation(a0_sb[:, h, HALF:], a0[1][h], ACT.Copy, scale=0.04)
         place_upper(1)
         nc.scalar.activation(board[1][:].indirect(list_q[:]), a0_sb[:, 1, :], ACT.Copy)
 

from contextlib import ExitStack

import concourse.mybir as mybir

K, T, J, I, R, C, Q = 512, 512, 256, 256, 512, 512, 1024
FLOPS = 2 * K * R * J + 2 * K * R * I + 2 * R * J * I

F32 = mybir.dt.float32
BF16 = mybir.dt.bfloat16
I32 = mybir.dt.int32
U32 = mybir.dt.uint32
U16 = mybir.dt.uint16
U8 = mybir.dt.uint8
E4M3 = mybir.dt.float8_e4m3fn_x4
E5M2 = mybir.dt.float8_e5m2_x4
E2M1 = mybir.dt.float4_e2m1fn_x4
ALU = mybir.AluOpType
ACT = mybir.ActivationFunctionType

P = 128
PACK = 4
HALF = 128


def tile_list_meet_peakgated_timestable_placed_kernel(
    tc, xt_words, xt_scales, wa_words, wa_scales, wb_words, wb_scales, tf, old, offs, offs2, offs3, offs4, out
):
    nc = tc.nc
    with ExitStack() as ctx:
        sb = ctx.enter_context(tc.tile_pool(name="sb", bufs=1))
        ps = ctx.enter_context(tc.psum_pool(name="ps", bufs=1))

        def load_list(src, name):
            t = sb.tile([P, 16], U16, name=name)
            nc.sync.dma_start(t[:], src)
            return t

        def load_scales(src, name, queue):
            t = sb.tile([P, 512], U8, name=name, tag=name, align_bytes=64)
            rows = src[0].bitcast(I32)
            for quad in range(4):
                four = rows[4 * quad : 4 * quad + 4, :].unsqueeze(0).broadcast_to([8, 4, 128])
                queue.dma_start(t[32 * quad : 32 * quad + 32, :].bitcast(I32), four)
            return t

        def load_weight_scales(src, name):
            t = sb.tile([P, 512], U8, name=name, tag=name, align_bytes=64)
            nc.vector.memset(t[:].bitcast(I32), 0)
            rows = src[0].bitcast(I32)
            for quad in range(4):
                nc.sync.dma_start(t[32 * quad : 32 * quad + 4, :].bitcast(I32), rows[4 * quad : 4 * quad + 4, :])
            return t

        tf_rows = tf.rearrange("(g t e) c -> t g e c", t=4, e=8)
        tf_sb = [sb.tile([P, C], F32, name="tf%d" % t) for t in range(PACK)]

        xt_w = sb.tile([P, T], I32, name="xt_w", align_bytes=64)
        nc.sync.dma_start(xt_w[:], xt_words[0].rearrange("p n t -> p (n t)").bitcast(I32))
        list_j = load_list(offs, "list_j")
        list_i = load_list(offs2, "list_i")
        xt_s = load_scales(xt_scales, "xt_s", nc.sync)
        nc.sync.dma_start(tf_sb[0][:], tf_rows[0])
        list_c = load_list(offs3, "list_c")
        wa_w = sb.tile([P, R // 2], I32, name="wa_w", align_bytes=64)
        nc.sync.dma_start(wa_w[:], wa_words[0].bitcast(I32))
        wa_s = load_weight_scales(wa_scales, "wa_s")
        nc.sync.dma_start(tf_sb[1][:], tf_rows[1])
        nc.sync.dma_start(tf_sb[2][:], tf_rows[2])
        wb_w = sb.tile([P, R], I32, name="wb_w", align_bytes=64)
        nc.sync.dma_start(wb_w[:], wb_words[0].rearrange("p n t -> p (n t)").bitcast(I32))
        nc.sync.dma_start(tf_sb[3][:], tf_rows[3])
        wb_s = load_weight_scales(wb_scales, "wb_s")
        list_q = load_list(offs4, "list_q")
        old_sb = [sb.tile([P, Q], F32, name="old%d" % h) for h in range(2)]
        for h in range(2):
            nc.sync.dma_start(old_sb[h][:], old[h * P : (h + 1) * P, :])

        board = [sb.tile([P, Q], F32, name="board%d" % h) for h in range(2)]
        for h in range(2):
            nc.gpsimd.memset(board[h][:], 0.0)

        def gather_words(lst, name):
            w = sb.tile([P, 256], U32, name=name, align_bytes=64)
            nc.vector.tensor_copy(w[:], xt_w[:].bitcast(U32).indirect(lst[:]))
            return w

        def gather_scales(lst, name, tag):
            s = sb.tile([P, 256], U8, name=name, tag=tag, align_bytes=64)
            nc.vector.tensor_copy(s[:], xt_s[:].indirect(lst[:]))
            return s

        def deal(src, words, name, dtype, cols):
            dst = sb.tile([P, cols], dtype, name=name, align_bytes=64)
            nc.vector.tensor_copy(
                dst[:].bitcast(I32).rearrange("p (t q b) -> p t q b", t=4, b=words),
                src[:].bitcast(I32).rearrange("p (q t b) -> p t q b", t=4, b=words),
            )
            return dst

        xa_w = gather_words(list_j, "xa_w")
        xa_s = gather_scales(list_j, "xa_s", "xa_s")
        xb_w = gather_words(list_i, "xb_w")
        wa_d = deal(wa_w, 4, "wa_d", U8, 2 * R)
        wa_ds = deal(wa_s, 2, "wa_ds", U8, R)
        za = [ps.tile([P, J], F32, name="za%d" % t, tag="bank%d" % t) for t in range(PACK)]
        for t in range(PACK):
            nc.tensor.matmul_mx(
                out=za[t][:],
                lhsT=wa_d[:, 2 * P * t : 2 * P * (t + 1)].bitcast(E2M1),
                lhsT_scale=wa_ds[:, P * t : P * (t + 1)],
                rhs=xa_w[:].bitcast(E4M3),
                rhs_scale=xa_s[:],
                start=True,
                stop=True,
            )

        xb_s = gather_scales(list_i, "xb_s", "wa_s")
        wb_d = deal(wb_w, 8, "wb_d", U32, R)
        wb_ds = deal(wb_s, 2, "wb_ds", U8, R)
        zb = [ps.tile([P, PACK, HALF], F32, name="zb%d" % u) for u in range(2)]
        for u in range(2):
            for t in range(PACK):
                nc.tensor.matmul_mx(
                    out=zb[u][:, t, :],
                    lhsT=wb_d[:, P * t : P * (t + 1)].bitcast(E5M2),
                    lhsT_scale=wb_ds[:, P * t : P * (t + 1)],
                    rhs=xb_w[:, HALF * u : HALF * (u + 1)].bitcast(E4M3),
                    rhs_scale=xb_s[:, HALF * u : HALF * (u + 1)],
                    start=True,
                    stop=True,
                )

        tfg = [
            sb.tile([P, PACK, HALF], F32, name="tfg0", tag="tfg0"),
            None,
        ]

        def gather_factors(u, t):
            nc.scalar.activation(tfg[u][:, t, :], tf_sb[t][:].indirect(list_c[:, 8 * u : 8 * (u + 1)]), ACT.Copy)

        for t in range(PACK - 1):
            gather_factors(0, t)

        ha_rows = sb.tile([P, PACK, J], F32, name="ha_rows")
        scaled = sb.tile([P, PACK, J], F32, name="scaled")
        for t in range(PACK):
            neg_cut = sb.tile([P, 1], F32, name="neg_cut%d" % t, tag="neg_cut%d" % t)
            nc.vector.tensor_scalar(scaled[:, t, :], za[t][:], -0.4, None, ALU.mult, ALU.min, accum_out=neg_cut[:])
            nc.scalar.activation(ha_rows[:, t, :], za[t][:], ACT.Relu, bias=neg_cut[:])

        gather_factors(0, PACK - 1)
        tfg[1] = sb.tile([P, PACK, HALF], F32, name="tfg1", tag="neg_cut3")
        for t in range(PACK):
            gather_factors(1, t)

        hb_bf = sb.tile([P, HALF * PACK], BF16, name="hb_bf", align_bytes=64)
        hb_w = [sb.tile([P, HALF], U32, name="hb_w%d" % u, align_bytes=64) for u in range(2)]
        hb_s = [sb.tile([P, HALF], U8, name="hb_s%d" % u, align_bytes=64) for u in range(2)]

        def make_hb(u):
            nc.vector.tensor_tensor(
                hb_bf[:].rearrange("p (c i t) -> p c t i", i=2, t=4),
                zb[u][:].rearrange("p t (c i) -> p c t i", i=2),
                tfg[u][:].rearrange("p t (c i) -> p c t i", i=2),
                ALU.mult,
            )

        def quantise_hb(u):
            nc.vector.quantize_mx(out=hb_w[u][:].bitcast(E5M2), scales=hb_s[u][:], in_=hb_bf[:])

        make_hb(0)
        ha_bf = sb.tile([P, J * PACK], BF16, name="ha_bf", tag="wb_s", align_bytes=64)
        nc.vector.tensor_copy(
            ha_bf[:].rearrange("p (c i t) -> p c t i", i=2, t=4),
            ha_rows[:].rearrange("p t (c i) -> p c t i", i=2),
        )
        quantise_hb(0)
        ha_w = sb.tile([P, J], U32, name="ha_w", align_bytes=64)
        ha_s = sb.tile([P, J], U8, name="ha_s", align_bytes=64)
        nc.vector.quantize_mx(out=ha_w[:].bitcast(E4M3), scales=ha_s[:], in_=ha_bf[:])

        first_bank = ps.tile([P, 2, HALF], F32, name="a0_first")
        a0 = [
            [first_bank[:, h, :] for h in range(2)],
            [ps.tile([P, HALF], F32, name="a0_second%d" % h, tag="bank%d" % h)[:] for h in range(2)],
        ]
        a0_sb = sb.tile([P, 2, I], F32, name="a0_sb")

        def scores(u):
            for h in range(2):
                nc.tensor.matmul_mx(
                    out=a0[u][h],
                    lhsT=ha_w[:, P * h : P * (h + 1)].bitcast(E4M3),
                    lhsT_scale=ha_s[:, P * h : P * (h + 1)],
                    rhs=hb_w[u][:].bitcast(E5M2),
                    rhs_scale=hb_s[u][:],
                    start=True,
                    stop=True,
                )

        def place_upper(u):
            nc.vector.tensor_copy(
                board[0][:].indirect(list_q[:, 8 * u : 8 * (u + 1)]), a0_sb[:, 0, HALF * u : HALF * (u + 1)]
            )

        scores(0)
        nc.scalar.activation(a0_sb[:, :, :HALF], first_bank[:], ACT.Copy, scale=0.04)
        make_hb(1)
        quantise_hb(1)
        place_upper(0)
        scores(1)
        for h in range(2):
            nc.scalar.activation(a0_sb[:, h, HALF:], a0[1][h], ACT.Copy, scale=0.04)
        place_upper(1)
        nc.scalar.activation(board[1][:].indirect(list_q[:]), a0_sb[:, 1, :], ACT.Copy)

        for h, widths in ((0, (512, 512)), (1, (512, 512))):
            for n, width in enumerate(widths):
                c0 = sum(widths[:n])
                cols = slice(c0, c0 + width)
                res = sb.tile([P, width], F32, name="res%d_%d" % (h, c0))
                nc.vector.scalar_tensor_tensor(res[:], old_sb[h][:, cols], -0.04, board[h][:, cols], ALU.mult, ALU.add)
                nc.sync.dma_start(out[h * P : (h + 1) * P, cols], res[:])
